import numpy as np, ml_dtypes
CORES = [50,52,122,124]
N = 4
import mx_ref
NC = 256
A = np.float32(0.03)
BF = ml_dtypes.bfloat16
def setup_inputs(rng):
    def f(*shape):
        return mx_ref.flush((rng.standard_normal(shape, dtype=np.float32) * np.exp2(rng.integers(-2, 3, shape[:-1] + (1,)))).astype(BF))
    return {"x": f(N, 128, 512), "w": f(N, 128, 4 * NC)}
def setup_inputs_blocks(rng):
    d = setup_inputs(rng)
    for k in ("x", "w"): d[k] = mx_ref.spread(d[k], rng, 2)
    return d
def setup_inputs_sharp(rng):
    d = setup_inputs(rng); d["w"] = (d["w"].astype(np.float32) * 32).astype(BF)
    return d
def setup_inputs_apart(rng):
    d = setup_inputs(rng); d["w"] = mx_ref.flush((d["w"].astype(np.float32) * np.exp2(rng.permutation(np.linspace(-3, 3, N))).astype(np.float32).reshape(N, 1, 1)).astype(BF))
    return d
def reference(x, w):
    W = [mx_ref.quantize(w[r]) for r in range(N)]
    y = np.zeros((N, 128, N * NC), np.float32)
    for j in range(N):
        X = mx_ref.quantize(x[j])
        L = [(mx_ref.matmul(X, W[r]) * A).astype(np.float64) for r in range(N)]
        m = np.max([l.max(axis=1, keepdims=True) for l in L], axis=0); s = sum(np.exp(l - m).sum(axis=1, keepdims=True) for l in L)
        for r in range(N):
            y[r][:, NC * j:NC * j + NC] = (np.exp(L[r] - m) / s).astype(np.float32)
    return {"y": y}

@@ -1,0 +1,211 @@
+import numpy as np
+from concourse.bass import DstId, RemoteDMATransfer
+from concourse.mybir import dt, AluOpType, AxisListType, ActivationFunctionType
+
+N = 4
+NC = 256
+SCALE = float(np.float32(0.03))
+
+SCRATCH = {
+    "xb": ("sbuf", [128, 512], "bfloat16"),
+    "wb": ("sbuf", [128, 1024], "bfloat16"),
+    "xq": ("sbuf", [128, 128 * N], "float8_e4m3fn_x4"),
+    "xs": ("sbuf", [128, 128 * N], "uint8"),
+    "wq": ("sbuf", [128, 2 * NC], "float8_e4m3fn_x4"),
+    "ws": ("sbuf", [128, 2 * NC], "uint8"),
+    "ps": ("psum", [128, 512 * 2 * N], "float32"),
+    "e": ("sbuf", [128, NC * N], "float32"),
+    "junk": ("sbuf", [128, NC * N], "float32"),
+    "tm": ("sbuf", [128, 8], "float32"),
+    "Q": ("sbuf", [128, 36], "float32"),
+    "d8": ("sbuf", [128, 8], "float32"),
+    "D8": ("sbuf", [128, 8], "float32"),
+    "E8": ("sbuf", [128, 8], "float32"),
+    "SC": ("sbuf", [128, 8], "float32"),
+    "P8": ("sbuf", [128, 8], "float32"),
+    "S4": ("sbuf", [128, 4], "float32"),
+    "r4": ("sbuf", [128, 4], "float32"),
+    "f4": ("sbuf", [128, 4], "float32"),
+}
+SEMAPHORES = (["ldx", "ldw", "qx", "qw", "wc", "wz", "st", "ls", "dup", "scv", "v1", "dd", "ee", "p8", "s4", "r4",
+               "ff", "fin0", "fin1", "sto"]
+              + ["%s%d" % (n, j) for n in ("xc", "xz", "ma", "mb", "rd", "nm", "ex") for j in range(N)])
+
+
+def _eng(m):
+    return [b for b in range(m.bit_length()) if (m >> b) & 1]
+
+
+def _msk(engines):
+    return sum(1 << b for b in engines)
+
+
+def rank_program(g, core, T, topo):
+    r = T.rank_of(core)
+    if r is None:
+        return
+    cores = list(T.cores)
+    sem = T.sem
+    mine = [c for c in cores if topo.chip(c) == topo.chip(core)]
+    far = [c for c in cores if topo.chip(c) != topo.chip(core)]
+
+    def lead_of(group, others):
+        return [c for c in group if all(topo.may_write(c, d) for d in others)][0]
+
+    my_lead, far_lead = lead_of(mine, far), lead_of(far, mine)
+    partner = [c for c in mine if c != core][0]
+    far_other = [c for c in far if c != far_lead][0]
+    is_lead = core == my_lead
+    p, rl, rn = T.rank_of(partner), T.rank_of(far_lead), T.rank_of(far_other)
+    order = [r, p, rl, rn]
+
+    def engine_sets(lead, lead_partner, other_lead):
+        off = _eng(topo.mask(lead, other_lead))
+        al = _eng(topo.mask(lead, lead_partner))
+        return off, al, [b for b in al if b not in off]
+
+    my_other = [c for c in mine if c != my_lead][0]
+    off, al, hi = engine_sets(my_lead, my_other, far_lead)
+    foff, _fal, _fhi = engine_sets(far_lead, far_other, my_lead)
+    up = _eng(topo.mask(my_other, my_lead))
+
+    if is_lead:
+        n_x = {p: len(up), rl: len(foff), rn: len(foff)}
+        n_w = len(up)
+    else:
+        n_x = {p: len(hi), rl: len(hi), rn: len(al)}
+        n_w = len(hi)
+    n_st = len(foff)
+
+    def xc(j):
+        return T.xq[:, 128 * j:128 * j + 128].bitcast(dt.uint8)
+
+    def xz(j):
+        return T.xs[:, 128 * j:128 * j + 128]
+
+    def did(c):
+        rid, pid, _ = topo.addr(c)
+        return DstId(rid=rid, pnc=pid)
+
+    sent = [0]
+
+    def send(parts):
+        trs = []
+        for src, dst, tos, engines, s in parts:
+            trs.append(RemoteDMATransfer(dst_ids=[did(c) for c in tos], dma_engine_mask=_msk(engines), remote_sem=s,
+                                         srcs=[src], dsts=[dst for _ in tos]))
+            sent[0] += len(engines)
+        g.remote_dma_fused(trs, local_sem=sem.ls)
+
+    g.sync.dma_start(T.xb[:], T.x[:]).then_inc(sem.ldx, 16)
+    g.sync.dma_start(T.wb[:], T.w[:]).then_inc(sem.ldw, 16)
+
+    g.wait_ge(sem.qx, 1)
+    if is_lead:
+        send([(xc(r), xc(r), [far_lead], off, sem["xc%d" % r]), (xc(r), xc(r), [partner], hi, sem["xc%d" % r])])
+        send([(xz(r), xz(r), [far_lead], off, sem["xz%d" % r]), (xz(r), xz(r), [partner], hi, sem["xz%d" % r])])
+        w_eng = hi
+    else:
+        send([(xc(r), xc(r), [my_lead], up, sem["xc%d" % r])])
+        send([(xz(r), xz(r), [my_lead], up, sem["xz%d" % r])])
+        w_eng = up
+    g.wait_ge(sem.qw, 1)
+    send([(T.wq[:, 0:NC].bitcast(dt.uint8), T.wq[:, NC:2 * NC].bitcast(dt.uint8), [partner], w_eng, sem.wc)])
+    send([(T.ws[:, 0:NC], T.ws[:, NC:2 * NC], [partner], w_eng, sem.wz)])
+    if is_lead:
+        g.wait_ge(sem["xc%d" % p], n_x[p])
+        send([(xc(p), xc(p), [far_lead], off, sem["xc%d" % p])])
+        g.wait_ge(sem["xz%d" % p], n_x[p])
+        send([(xz(p), xz(p), [far_lead], off, sem["xz%d" % p])])
+        for j, engines in ((rl, hi), (rn, al)):
+            g.wait_ge(sem["xc%d" % j], n_x[j])
+            send([(xc(j), xc(j), [partner], engines, sem["xc%d" % j])])
+            g.wait_ge(sem["xz%d" % j], n_x[j])
+            send([(xz(j), xz(j), [partner], engines, sem["xz%d" % j])])
+        for j in order:
+            g.wait_ge(sem["ex%d" % j], 2)
+        g.wait_ge(sem.dup, 2)
+        send([(T.Q[:, 0:16], T.Q[:, 16:32], [far_lead, far_other], off, sem.st)])
+    g.wait_ge(sem.ls, sent[0])
+
+    t = g.tensor
+    t.wait_ge(sem.qw, 1)
+    for k, j in enumerate(order):
+        if j == r:
+            t.wait_ge(sem.qx, 1)
+        else:
+            t.wait_ge(sem["xc%d" % j], n_x[j])
+            t.wait_ge(sem["xz%d" % j], n_x[j])
+        X, XS = T.xq[:, 128 * j:128 * j + 128], T.xs[:, 128 * j:128 * j + 128]
+        t.matmul_mx(T.ps[:, 1024 * j:1024 * j + NC], X, XS, T.wq[:, 0:NC], T.ws[:, 0:NC], True, True
+                    ).then_inc(sem["ma%d" % j], 1)
+        if k == 0:
+            t.wait_ge(sem.wc, n_w)
+            t.wait_ge(sem.wz, n_w)
+        t.matmul_mx(T.ps[:, 1024 * j + 512:1024 * j + 512 + NC], X, XS, T.wq[:, NC:2 * NC], T.ws[:, NC:2 * NC],
+                    True, True).then_inc(sem["mb%d" % j], 1)
+
+    v = g.vector
+    Q = T.Q
+    v.wait_ge(sem.ldx, 16)
+    v.quantize_mx(T.xq[:, 128 * r:128 * r + 128], T.xs[:, 128 * r:128 * r + 128], T.xb[:]).then_inc(sem.qx, 1)
+    v.wait_ge(sem.ldw, 16)
+    v.quantize_mx(T.wq[:, 0:NC], T.ws[:, 0:NC], T.wb[:]).then_inc(sem.qw, 1)
+    for j in order:
+        v.wait_ge(sem["ma%d" % j], 1)
+        v.tensor_reduce(T.tm[:, j:j + 1], T.ps[:, 1024 * j:1024 * j + NC], AxisListType.X, AluOpType.max,
+                        negate=True).then_inc(sem["rd%d" % j], 1)
+        v.wait_ge(sem["mb%d" % j], 1)
+        v.tensor_reduce(T.tm[:, 4 + j:5 + j], T.ps[:, 1024 * j + 512:1024 * j + 512 + NC], AxisListType.X,
+                        AluOpType.max, negate=True).then_inc(sem["rd%d" % j], 1)
+        v.wait_ge(sem["rd%d" % j], 2)
+        v.tensor_scalar(Q[:, j:j + 1], T.tm[:, 4 + j:5 + j], T.tm[:, j:j + 1], SCALE, AluOpType.min, AluOpType.mult
+                        ).then_inc(sem["nm%d" % j], 1)
+    for j in order:
+        v.wait_ge(sem["nm%d" % j], 1)
+    v.tensor_copy(Q[:, 12:16], Q[:, 0:4]).then_inc(sem.dup, 1)
+    v.tensor_copy(Q[:, 32:36], Q[:, 0:4]).then_inc(sem.dup, 1)
+    for j in order:
+        v.wait_ge(sem["ex%d" % j], 2)
+    v.tensor_tensor(T.SC[:, 0:4], Q[:, 4:8], Q[:, 8:12], AluOpType.add).then_inc(sem.scv, 1)
+    v.wait_ge(sem.dup, 2)
+    v.wait_ge(sem.st, n_st)
+    v.tensor_tensor(T.d8[:], Q[:, 28:36], Q[:, 12:20], AluOpType.subtract).then_inc(sem.v1, 1)
+    v.wait_ge(sem.v1, 1)
+    v.tensor_scalar(T.D8[:], T.d8[:], 0.0, None, AluOpType.min).then_inc(sem.dd, 1)
+    v.tensor_tensor(T.SC[:, 4:8], Q[:, 20:24], Q[:, 24:28], AluOpType.add).then_inc(sem.scv, 1)
+    v.wait_ge(sem.scv, 2)
+    v.wait_ge(sem.ee, 1)
+    v.tensor_tensor(T.P8[:], T.E8[:], T.SC[:], AluOpType.mult).then_inc(sem.p8, 1)
+    v.wait_ge(sem.p8, 1)
+    v.tensor_tensor(T.S4[:], T.P8[:, 0:4], T.P8[:, 4:8], AluOpType.add).then_inc(sem.s4, 1)
+    v.wait_ge(sem.s4, 1)
+    v.reciprocal(T.r4[:], T.S4[:]).then_inc(sem.r4, 1)
+    v.wait_ge(sem.r4, 1)
+    v.tensor_tensor(T.f4[:], T.E8[:, 0:4], T.r4[:], AluOpType.mult).then_inc(sem.ff, 1)
+    v.wait_ge(sem.ff, 1)
+    for j, s in ((0, sem.fin0), (2, sem.fin1)):
+        v.tensor_scalar(T.e[:, NC * j:NC * j + NC], T.e[:, NC * j:NC * j + NC], T.f4[:, j:j + 1], None, AluOpType.mult
+                        ).then_inc(s, 1)
+
+    a = g.scalar
+    for j in order:
+        a.wait_ge(sem["nm%d" % j], 1)
+        a.activation(T.e[:, NC * j:NC * j + NC], T.ps[:, 1024 * j:1024 * j + NC], ActivationFunctionType.Exp,
+                     bias=Q[:, j:j + 1], scale=SCALE, accum_out=Q[:, 4 + j:5 + j]).then_inc(sem["ex%d" % j], 1)
+        a.activation(T.junk[:, NC * j:NC * j + NC], T.ps[:, 1024 * j + 512:1024 * j + 512 + NC],
+                     ActivationFunctionType.Exp, bias=Q[:, j:j + 1], scale=SCALE, accum_out=Q[:, 8 + j:9 + j]
+                     ).then_inc(sem["ex%d" % j], 1)
+    a.wait_ge(sem.dd, 1)
+    a.activation(T.E8[:], T.D8[:], ActivationFunctionType.Exp).then_inc(sem.ee, 1)
+    a.wait_ge(sem.ff, 1)
+    for j, s in ((1, sem.fin0), (3, sem.fin1)):
+        a.wait_ge(sem["ex%d" % j], 2)
+        a.activation(T.e[:, NC * j:NC * j + NC], T.e[:, NC * j:NC * j + NC], ActivationFunctionType.Copy,
+                     scale=T.f4[:, j:j + 1]).then_inc(s, 1)
+
+    g.sync.wait_ge(sem.fin0, 2)
+    g.sync.dma_start(T.y[:, 0:2 * NC], T.e[:, 0:2 * NC]).then_inc(sem.sto, 16)
+    g.sync.wait_ge(sem.fin1, 2)
+    g.sync.dma_start(T.y[:, 2 * NC:4 * NC], T.e[:, 2 * NC:4 * NC]).then_inc(sem.sto, 16)
+    g.sync.wait_ge(sem.sto, 32)

@@ -5,6 +5,7 @@ from concourse.mybir import dt, AluOpType, AxisListType, ActivationFunctionType
 N = 4
 NC = 256
 SCALE = float(np.float32(0.03))
+CAP = 80.0
 
 SCRATCH = {
     "xb": ("sbuf", [128, 512], "bfloat16"),
@@ -16,20 +17,22 @@ SCRATCH = {
     "ps": ("psum", [128, 512 * 2 * N], "float32"),
     "e": ("sbuf", [128, NC * N], "float32"),
     "junk": ("sbuf", [128, NC * N], "float32"),
-    "tm": ("sbuf", [128, 8], "float32"),
-    "Q": ("sbuf", [128, 36], "float32"),
-    "d8": ("sbuf", [128, 8], "float32"),
-    "D8": ("sbuf", [128, 8], "float32"),
-    "E8": ("sbuf", [128, 8], "float32"),
-    "SC": ("sbuf", [128, 8], "float32"),
-    "P8": ("sbuf", [128, 8], "float32"),
+    "sc": ("sbuf", [128, NC * 2 * N], "float32"),
+    "cv": ("sbuf", [128, NC], "float32"),
+    "Q": ("sbuf", [128, 32], "float32"),
+    "M4": ("sbuf", [128, 4], "float32"),
+    "R": ("sbuf", [128, 24], "float32"),
+    "d": ("sbuf", [128, 24], "float32"),
+    "D": ("sbuf", [128, 24], "float32"),
+    "E": ("sbuf", [128, 24], "float32"),
+    "P": ("sbuf", [128, 24], "float32"),
+    "U": ("sbuf", [128, 8], "float32"),
     "S4": ("sbuf", [128, 4], "float32"),
     "r4": ("sbuf", [128, 4], "float32"),
-    "f4": ("sbuf", [128, 4], "float32"),
 }
-SEMAPHORES = (["ldx", "ldw", "qx", "qw", "wc", "wz", "st", "ls", "dup", "scv", "v1", "dd", "ee", "p8", "s4", "r4",
-               "ff", "fin0", "fin1", "sto"]
-              + ["%s%d" % (n, j) for n in ("xc", "xz", "ma", "mb", "rd", "nm", "ex") for j in range(N)])
+SEMAPHORES = (["ldx", "ldw", "qx", "qw", "wc", "wz", "st", "sl", "ls", "ms", "cp", "rr", "v1", "dd", "ee", "p8", "u8",
+               "s4", "r4", "fin0", "fin1", "sto"]
+              + ["%s%d" % (n, j) for n in ("xc", "xz", "ma", "mb", "na", "nb", "ex") for j in range(N)])
 
 
 def _eng(m):
@@ -41,41 +44,25 @@ def _msk(engines):
 
 
 def rank_program(g, core, T, topo):
-    r = T.rank_of(core)
-    if r is None:
-        return
     cores = list(T.cores)
     sem = T.sem
     mine = [c for c in cores if topo.chip(c) == topo.chip(core)]
+    if not mine:
+        return
     far = [c for c in cores if topo.chip(c) != topo.chip(core)]
 
     def lead_of(group, others):
         return [c for c in group if all(topo.may_write(c, d) for d in others)][0]
 
+    def helper_of(other, others):
+        return [c for c in range(topo.CORES_PER_CHIP * topo.CHIPS)
+                if c not in cores and topo.chip(c) == topo.chip(other) and topo.die(c) == topo.die(other)
+                and all(topo.may_write(c, d) for d in others)][0]
+
     my_lead, far_lead = lead_of(mine, far), lead_of(far, mine)
-    partner = [c for c in mine if c != core][0]
-    far_other = [c for c in far if c != far_lead][0]
-    is_lead = core == my_lead
-    p, rl, rn = T.rank_of(partner), T.rank_of(far_lead), T.rank_of(far_other)
-    order = [r, p, rl, rn]
-
-    def engine_sets(lead, lead_partner, other_lead):
-        off = _eng(topo.mask(lead, other_lead))
-        al = _eng(topo.mask(lead, lead_partner))
-        return off, al, [b for b in al if b not in off]
-
     my_other = [c for c in mine if c != my_lead][0]
-    off, al, hi = engine_sets(my_lead, my_other, far_lead)
-    foff, _fal, _fhi = engine_sets(far_lead, far_other, my_lead)
-    up = _eng(topo.mask(my_other, my_lead))
-
-    if is_lead:
-        n_x = {p: len(up), rl: len(foff), rn: len(foff)}
-        n_w = len(up)
-    else:
-        n_x = {p: len(hi), rl: len(hi), rn: len(al)}
-        n_w = len(hi)
-    n_st = len(foff)
+    far_other = [c for c in far if c != far_lead][0]
+    my_helper, far_helper = helper_of(my_other, far), helper_of(far_other, mine)
 
     def xc(j):
         return T.xq[:, 128 * j:128 * j + 128].bitcast(dt.uint8)
@@ -97,112 +84,176 @@ def rank_program(g, core, T, topo):
             sent[0] += len(engines)
         g.remote_dma_fused(trs, local_sem=sem.ls)
 
+    up = _eng(topo.mask(my_other, my_lead))
+    upx = up[0::2]
+    uph = [b for b in _eng(topo.mask(my_other, my_helper)) if b not in upx][:len(upx)]
+
+    if core == my_helper:
+        j = T.rank_of(my_other)
+        out = _eng(topo.mask(core, far_other))
+        g.wait_ge(sem["xc%d" % j], len(uph))
+        send([(xc(j), xc(j), [far_other], out, sem["xc%d" % j])])
+        g.wait_ge(sem["xz%d" % j], len(uph))
+        send([(xz(j), xz(j), [far_other], out, sem["xz%d" % j])])
+        g.wait_ge(sem.ls, sent[0])
+        return
+    r = T.rank_of(core)
+    if r is None:
+        return
+
+    partner = [c for c in mine if c != core][0]
+    is_lead = core == my_lead
+    p, rl, rn = T.rank_of(partner), T.rank_of(far_lead), T.rank_of(far_other)
+    order = [r, p, rl, rn]
+
+    def engine_sets(lead, lead_partner, other_lead):
+        off = _eng(topo.mask(lead, other_lead))
+        al = _eng(topo.mask(lead, lead_partner))
+        return off, al, [b for b in al if b not in off]
+
+    off, al, hi = engine_sets(my_lead, my_other, far_lead)
+    foff, _fal, _fhi = engine_sets(far_lead, far_other, my_lead)
+
+    if is_lead:
+        n_x = {p: len(upx), rl: len(foff), rn: len(foff)}
+    else:
+        n_x = {p: len(hi), rl: len(hi), rn: len(_eng(topo.mask(far_helper, core)))}
+    n_w = len(up)
+    n_st = len(foff)
+    n_sl = len(hi)
+
+    if is_lead:
+        seq = [(r, 0), (p, 0), (r, 1), (p, 1), (rl, 0), (rl, 1), (rn, 0), (rn, 1)]
+    else:
+        seq = [(j, 0) for j in order]
+    n_ex = 2 if is_lead else 1
+
+    def msem(j, b):
+        return sem["%s%d" % ("mb" if b else "ma", j)]
+
+    def nsem(j, b):
+        return sem["%s%d" % ("nb" if b else "na", j)]
+
+    def bank(j, b):
+        return T.ps[:, 1024 * j + 512 * b:1024 * j + 512 * b + NC]
+
+    def shift(k):
+        return T.sc[:, NC * k + NC - 1:NC * k + NC]
+
     g.sync.dma_start(T.xb[:], T.x[:]).then_inc(sem.ldx, 16)
     g.sync.dma_start(T.wb[:], T.w[:]).then_inc(sem.ldw, 16)
 
+    Q = T.Q
     g.wait_ge(sem.qx, 1)
     if is_lead:
         send([(xc(r), xc(r), [far_lead], off, sem["xc%d" % r]), (xc(r), xc(r), [partner], hi, sem["xc%d" % r])])
         send([(xz(r), xz(r), [far_lead], off, sem["xz%d" % r]), (xz(r), xz(r), [partner], hi, sem["xz%d" % r])])
-        w_eng = hi
-    else:
-        send([(xc(r), xc(r), [my_lead], up, sem["xc%d" % r])])
-        send([(xz(r), xz(r), [my_lead], up, sem["xz%d" % r])])
-        w_eng = up
-    g.wait_ge(sem.qw, 1)
-    send([(T.wq[:, 0:NC].bitcast(dt.uint8), T.wq[:, NC:2 * NC].bitcast(dt.uint8), [partner], w_eng, sem.wc)])
-    send([(T.ws[:, 0:NC], T.ws[:, NC:2 * NC], [partner], w_eng, sem.wz)])
-    if is_lead:
         g.wait_ge(sem["xc%d" % p], n_x[p])
         send([(xc(p), xc(p), [far_lead], off, sem["xc%d" % p])])
         g.wait_ge(sem["xz%d" % p], n_x[p])
         send([(xz(p), xz(p), [far_lead], off, sem["xz%d" % p])])
-        for j, engines in ((rl, hi), (rn, al)):
-            g.wait_ge(sem["xc%d" % j], n_x[j])
-            send([(xc(j), xc(j), [partner], engines, sem["xc%d" % j])])
-            g.wait_ge(sem["xz%d" % j], n_x[j])
-            send([(xz(j), xz(j), [partner], engines, sem["xz%d" % j])])
+        g.wait_ge(sem["xc%d" % rl], n_x[rl])
+        send([(xc(rl), xc(rl), [partner], hi, sem["xc%d" % rl])])
+        g.wait_ge(sem["xz%d" % rl], n_x[rl])
+        send([(xz(rl), xz(rl), [partner], hi, sem["xz%d" % rl])])
+        g.wait_ge(sem.cp, len(seq))
         for j in order:
-            g.wait_ge(sem["ex%d" % j], 2)
-        g.wait_ge(sem.dup, 2)
-        send([(T.Q[:, 0:16], T.Q[:, 16:32], [far_lead, far_other], off, sem.st)])
+            g.wait_ge(sem["ex%d" % j], n_ex)
+        send([(Q[:, 0:16], Q[:, 16:32], [far_lead, far_other], off, sem.st),
+              (Q[:, 0:16], Q[:, 0:16], [partner], hi, sem.sl)])
+    else:
+        send([(xc(r), xc(r), [my_lead], upx, sem["xc%d" % r]), (xc(r), xc(r), [my_helper], uph, sem["xc%d" % r])])
+        send([(xz(r), xz(r), [my_lead], upx, sem["xz%d" % r]), (xz(r), xz(r), [my_helper], uph, sem["xz%d" % r])])
+        g.wait_ge(sem.qw, 1)
+        send([(T.wq[:, 0:NC].bitcast(dt.uint8), T.wq[:, NC:2 * NC].bitcast(dt.uint8), [my_lead], up, sem.wc)])
+        send([(T.ws[:, 0:NC], T.ws[:, NC:2 * NC], [my_lead], up, sem.wz)])
     g.wait_ge(sem.ls, sent[0])
 
     t = g.tensor
     t.wait_ge(sem.qw, 1)
-    for k, j in enumerate(order):
+    for j, b in seq:
         if j == r:
             t.wait_ge(sem.qx, 1)
         else:
             t.wait_ge(sem["xc%d" % j], n_x[j])
             t.wait_ge(sem["xz%d" % j], n_x[j])
-        X, XS = T.xq[:, 128 * j:128 * j + 128], T.xs[:, 128 * j:128 * j + 128]
-        t.matmul_mx(T.ps[:, 1024 * j:1024 * j + NC], X, XS, T.wq[:, 0:NC], T.ws[:, 0:NC], True, True
-                    ).then_inc(sem["ma%d" % j], 1)
-        if k == 0:
+        if b:
             t.wait_ge(sem.wc, n_w)
             t.wait_ge(sem.wz, n_w)
-        t.matmul_mx(T.ps[:, 1024 * j + 512:1024 * j + 512 + NC], X, XS, T.wq[:, NC:2 * NC], T.ws[:, NC:2 * NC],
-                    True, True).then_inc(sem["mb%d" % j], 1)
+        t.matmul_mx(bank(j, b), T.xq[:, 128 * j:128 * j + 128], T.xs[:, 128 * j:128 * j + 128],
+                    T.wq[:, NC * b:NC * b + NC], T.ws[:, NC * b:NC * b + NC], True, True).then_inc(msem(j, b), 1)
 
     v = g.vector
-    Q = T.Q
+    v.memset(T.cv[:, 0:NC - 1], 1.0).then_inc(sem.ms, 1)
+    v.memset(T.cv[:, NC - 1:NC], -SCALE).then_inc(sem.ms, 1)
+    v.memset(T.R[:, 8:16], 0.0).then_inc(sem.ms, 1)
     v.wait_ge(sem.ldx, 16)
     v.quantize_mx(T.xq[:, 128 * r:128 * r + 128], T.xs[:, 128 * r:128 * r + 128], T.xb[:]).then_inc(sem.qx, 1)
     v.wait_ge(sem.ldw, 16)
     v.quantize_mx(T.wq[:, 0:NC], T.ws[:, 0:NC], T.wb[:]).then_inc(sem.qw, 1)
+    v.wait_ge(sem.ms, 3)
+    own4 = Q[:, 0:4] if is_lead else T.M4[:]
+
+    def put(k):
+        j, b = seq[k]
+        v.wait_ge(nsem(j, b), 1)
+        dst = Q[:, 4 * b + j:4 * b + j + 1] if is_lead else T.M4[:, j:j + 1]
+        v.tensor_copy(dst, shift(k)).then_inc(sem.cp, 1)
+
+    todo = []
+    for k, (j, b) in enumerate(seq):
+        if k < len(seq) - 1:
+            for q in todo:
+                put(q)
+            todo = []
+        v.wait_ge(msem(j, b), 1)
+        v.tensor_tensor_scan(T.sc[:, NC * k:NC * k + NC], bank(j, b), T.cv[:], -1.0e29, AluOpType.max, AluOpType.mult
+                             ).then_inc(nsem(j, b), 1)
+        todo.append(k)
+    for q in todo:
+        put(q)
+    v.wait_ge(sem.cp, len(seq))
+    for c in (0, 4, 16, 20):
+        v.tensor_copy(T.R[:, c:c + 4], own4).then_inc(sem.rr, 1)
+    v.wait_ge(sem.rr, 4)
     for j in order:
-        v.wait_ge(sem["ma%d" % j], 1)
-        v.tensor_reduce(T.tm[:, j:j + 1], T.ps[:, 1024 * j:1024 * j + NC], AxisListType.X, AluOpType.max,
-                        negate=True).then_inc(sem["rd%d" % j], 1)
-        v.wait_ge(sem["mb%d" % j], 1)
-        v.tensor_reduce(T.tm[:, 4 + j:5 + j], T.ps[:, 1024 * j + 512:1024 * j + 512 + NC], AxisListType.X,
-                        AluOpType.max, negate=True).then_inc(sem["rd%d" % j], 1)
-        v.wait_ge(sem["rd%d" % j], 2)
-        v.tensor_scalar(Q[:, j:j + 1], T.tm[:, 4 + j:5 + j], T.tm[:, j:j + 1], SCALE, AluOpType.min, AluOpType.mult
-                        ).then_inc(sem["nm%d" % j], 1)
-    for j in order:
-        v.wait_ge(sem["nm%d" % j], 1)
-    v.tensor_copy(Q[:, 12:16], Q[:, 0:4]).then_inc(sem.dup, 1)
-    v.tensor_copy(Q[:, 32:36], Q[:, 0:4]).then_inc(sem.dup, 1)
-    for j in order:
-        v.wait_ge(sem["ex%d" % j], 2)
-    v.tensor_tensor(T.SC[:, 0:4], Q[:, 4:8], Q[:, 8:12], AluOpType.add).then_inc(sem.scv, 1)
-    v.wait_ge(sem.dup, 2)
+        v.wait_ge(sem["ex%d" % j], n_ex)
+    if not is_lead:
+        v.wait_ge(sem.sl, n_sl)
     v.wait_ge(sem.st, n_st)
-    v.tensor_tensor(T.d8[:], Q[:, 28:36], Q[:, 12:20], AluOpType.subtract).then_inc(sem.v1, 1)
+    v.tensor_tensor(T.d[:], T.R[:], Q[:, 0:24], AluOpType.subtract).then_inc(sem.v1, 1)
     v.wait_ge(sem.v1, 1)
-    v.tensor_scalar(T.D8[:], T.d8[:], 0.0, None, AluOpType.min).then_inc(sem.dd, 1)
-    v.tensor_tensor(T.SC[:, 4:8], Q[:, 20:24], Q[:, 24:28], AluOpType.add).then_inc(sem.scv, 1)
-    v.wait_ge(sem.scv, 2)
+    v.tensor_scalar(T.D[:], T.d[:], CAP, None, AluOpType.min).then_inc(sem.dd, 1)
     v.wait_ge(sem.ee, 1)
-    v.tensor_tensor(T.P8[:], T.E8[:], T.SC[:], AluOpType.mult).then_inc(sem.p8, 1)
+    v.tensor_tensor(T.P[:], T.E[:], Q[:, 8:32], AluOpType.mult).then_inc(sem.p8, 1)
     v.wait_ge(sem.p8, 1)
-    v.tensor_tensor(T.S4[:], T.P8[:, 0:4], T.P8[:, 4:8], AluOpType.add).then_inc(sem.s4, 1)
+    v.tensor_tensor(T.U[:], T.P[:, 0:8], T.P[:, 16:24], AluOpType.add).then_inc(sem.u8, 1)
+    v.wait_ge(sem.u8, 1)
+    v.tensor_tensor(T.S4[:], T.U[:, 0:4], T.U[:, 4:8], AluOpType.add).then_inc(sem.s4, 1)
     v.wait_ge(sem.s4, 1)
     v.reciprocal(T.r4[:], T.S4[:]).then_inc(sem.r4, 1)
     v.wait_ge(sem.r4, 1)
-    v.tensor_tensor(T.f4[:], T.E8[:, 0:4], T.r4[:], AluOpType.mult).then_inc(sem.ff, 1)
-    v.wait_ge(sem.ff, 1)
     for j, s in ((0, sem.fin0), (2, sem.fin1)):
-        v.tensor_scalar(T.e[:, NC * j:NC * j + NC], T.e[:, NC * j:NC * j + NC], T.f4[:, j:j + 1], None, AluOpType.mult
+        v.tensor_scalar(T.e[:, NC * j:NC * j + NC], T.e[:, NC * j:NC * j + NC], T.r4[:, j:j + 1], None, AluOpType.mult
                         ).then_inc(s, 1)
 
     a = g.scalar
-    for j in order:
-        a.wait_ge(sem["nm%d" % j], 1)
-        a.activation(T.e[:, NC * j:NC * j + NC], T.ps[:, 1024 * j:1024 * j + NC], ActivationFunctionType.Exp,
-                     bias=Q[:, j:j + 1], scale=SCALE, accum_out=Q[:, 4 + j:5 + j]).then_inc(sem["ex%d" % j], 1)
-        a.activation(T.junk[:, NC * j:NC * j + NC], T.ps[:, 1024 * j + 512:1024 * j + 512 + NC],
-                     ActivationFunctionType.Exp, bias=Q[:, j:j + 1], scale=SCALE, accum_out=Q[:, 8 + j:9 + j]
-                     ).then_inc(sem["ex%d" % j], 1)
+    for k, (j, b) in enumerate(seq):
+        a.wait_ge(nsem(j, b), 1)
+        out = (T.junk if b else T.e)[:, NC * j:NC * j + NC]
+        if is_lead:
+            a.activation(out, bank(j, b), ActivationFunctionType.Exp, bias=shift(k), scale=SCALE,
+                         accum_out=Q[:, 8 + 4 * b + j:9 + 4 * b + j]).then_inc(sem["ex%d" % j], 1)
+        else:
+            a.activation(out, bank(j, b), ActivationFunctionType.Exp, bias=shift(k), scale=SCALE
+                         ).then_inc(sem["ex%d" % j], 1)
     a.wait_ge(sem.dd, 1)
-    a.activation(T.E8[:], T.D8[:], ActivationFunctionType.Exp).then_inc(sem.ee, 1)
-    a.wait_ge(sem.ff, 1)
+    a.activation(T.E[:], T.D[:], ActivationFunctionType.Exp).then_inc(sem.ee, 1)
+    a.wait_ge(sem.r4, 1)
     for j, s in ((1, sem.fin0), (3, sem.fin1)):
-        a.wait_ge(sem["ex%d" % j], 2)
+        a.wait_ge(sem["ex%d" % j], n_ex)
         a.activation(T.e[:, NC * j:NC * j + NC], T.e[:, NC * j:NC * j + NC], ActivationFunctionType.Copy,
-                     scale=T.f4[:, j:j + 1]).then_inc(s, 1)
+                     scale=T.r4[:, j:j + 1]).then_inc(s, 1)
 
     g.sync.wait_ge(sem.fin0, 2)
     g.sync.dma_start(T.y[:, 0:2 * NC], T.e[:, 0:2 * NC]).then_inc(sem.sto, 16)

import numpy as np
from concourse.bass import DstId, RemoteDMATransfer
from concourse.mybir import dt, AluOpType, AxisListType, ActivationFunctionType

N = 4
NC = 256
SCALE = float(np.float32(0.03))
CAP = 80.0

SCRATCH = {
    "xb": ("sbuf", [128, 512], "bfloat16"),
    "wb": ("sbuf", [128, 1024], "bfloat16"),
    "xq": ("sbuf", [128, 128 * N], "float8_e4m3fn_x4"),
    "xs": ("sbuf", [128, 128 * N], "uint8"),
    "wq": ("sbuf", [128, 2 * NC], "float8_e4m3fn_x4"),
    "ws": ("sbuf", [128, 2 * NC], "uint8"),
    "ps": ("psum", [128, 512 * 2 * N], "float32"),
    "e": ("sbuf", [128, NC * N], "float32"),
    "junk": ("sbuf", [128, NC * N], "float32"),
    "sc": ("sbuf", [128, NC * 2 * N], "float32"),
    "cv": ("sbuf", [128, NC], "float32"),
    "Q": ("sbuf", [128, 32], "float32"),
    "M4": ("sbuf", [128, 4], "float32"),
    "R": ("sbuf", [128, 24], "float32"),
    "d": ("sbuf", [128, 24], "float32"),
    "D": ("sbuf", [128, 24], "float32"),
    "E": ("sbuf", [128, 24], "float32"),
    "P": ("sbuf", [128, 24], "float32"),
    "U": ("sbuf", [128, 8], "float32"),
    "S4": ("sbuf", [128, 4], "float32"),
    "r4": ("sbuf", [128, 4], "float32"),
}
SEMAPHORES = (["ldx", "ldw", "qx", "qw", "wc", "wz", "st", "sl", "ls", "ms", "cp", "rr", "v1", "dd", "ee", "p8", "u8",
               "s4", "r4", "fin0", "fin1", "sto"]
              + ["%s%d" % (n, j) for n in ("xc", "xz", "ma", "mb", "na", "nb", "ex") for j in range(N)])


def _eng(m):
    return [b for b in range(m.bit_length()) if (m >> b) & 1]


def _msk(engines):
    return sum(1 << b for b in engines)


def rank_program(g, core, T, topo):
    cores = list(T.cores)
    sem = T.sem
    mine = [c for c in cores if topo.chip(c) == topo.chip(core)]
    if not mine:
        return
    far = [c for c in cores if topo.chip(c) != topo.chip(core)]

    def lead_of(group, others):
        return [c for c in group if all(topo.may_write(c, d) for d in others)][0]

    def helper_of(other, others):
        return [c for c in range(topo.CORES_PER_CHIP * topo.CHIPS)
                if c not in cores and topo.chip(c) == topo.chip(other) and topo.die(c) == topo.die(other)
                and all(topo.may_write(c, d) for d in others)][0]

    my_lead, far_lead = lead_of(mine, far), lead_of(far, mine)
    my_other = [c for c in mine if c != my_lead][0]
    far_other = [c for c in far if c != far_lead][0]
    my_helper, far_helper = helper_of(my_other, far), helper_of(far_other, mine)

    def xc(j):
        return T.xq[:, 128 * j:128 * j + 128].bitcast(dt.uint8)

    def xz(j):
        return T.xs[:, 128 * j:128 * j + 128]

    def did(c):
        rid, pid, _ = topo.addr(c)
        return DstId(rid=rid, pnc=pid)

    sent = [0]

    def send(parts):
        trs = []
        for src, dst, tos, engines, s in parts:
            trs.append(RemoteDMATransfer(dst_ids=[did(c) for c in tos], dma_engine_mask=_msk(engines), remote_sem=s,
                                         srcs=[src], dsts=[dst for _ in tos]))
            sent[0] += len(engines)
        g.remote_dma_fused(trs, local_sem=sem.ls)

    up = _eng(topo.mask(my_other, my_lead))
    upx = up[0::2]
    uph = [b for b in _eng(topo.mask(my_other, my_helper)) if b not in upx][:len(upx)]

    if core == my_helper:
        j = T.rank_of(my_other)
        out = _eng(topo.mask(core, far_other))
        g.wait_ge(sem["xc%d" % j], len(uph))
        send([(xc(j), xc(j), [far_other], out, sem["xc%d" % j])])
        g.wait_ge(sem["xz%d" % j], len(uph))
        send([(xz(j), xz(j), [far_other], out, sem["xz%d" % j])])
        g.wait_ge(sem.ls, sent[0])
        return
    r = T.rank_of(core)
    if r is None:
        return

    partner = [c for c in mine if c != core][0]
    is_lead = core == my_lead
    p, rl, rn = T.rank_of(partner), T.rank_of(far_lead), T.rank_of(far_other)
    order = [r, p, rl, rn]

    def engine_sets(lead, lead_partner, other_lead):
        off = _eng(topo.mask(lead, other_lead))
        al = _eng(topo.mask(lead, lead_partner))
        return off, al, [b for b in al if b not in off]

    off, al, hi = engine_sets(my_lead, my_other, far_lead)
    foff, _fal, _fhi = engine_sets(far_lead, far_other, my_lead)

    if is_lead:
        n_x = {p: len(upx), rl: len(foff), rn: len(foff)}
    else:
        n_x = {p: len(hi), rl: len(hi), rn: len(_eng(topo.mask(far_helper, core)))}
    n_w = len(up)
    n_st = len(foff)
    n_sl = len(hi)

    if is_lead:
        seq = [(r, 0), (p, 0), (r, 1), (p, 1), (rl, 0), (rl, 1), (rn, 0), (rn, 1)]
    else:
        seq = [(j, 0) for j in order]
    n_ex = 2 if is_lead else 1

    def msem(j, b):
        return sem["%s%d" % ("mb" if b else "ma", j)]

    def nsem(j, b):
        return sem["%s%d" % ("nb" if b else "na", j)]

    def bank(j, b):
        return T.ps[:, 1024 * j + 512 * b:1024 * j + 512 * b + NC]

    def shift(k):
        return T.sc[:, NC * k + NC - 1:NC * k + NC]

    g.sync.dma_start(T.xb[:], T.x[:]).then_inc(sem.ldx, 16)
    g.sync.dma_start(T.wb[:], T.w[:]).then_inc(sem.ldw, 16)

    Q = T.Q
    g.wait_ge(sem.qx, 1)
    if is_lead:
        send([(xc(r), xc(r), [far_lead], off, sem["xc%d" % r]), (xc(r), xc(r), [partner], hi, sem["xc%d" % r])])
        send([(xz(r), xz(r), [far_lead], off, sem["xz%d" % r]), (xz(r), xz(r), [partner], hi, sem["xz%d" % r])])
        g.wait_ge(sem["xc%d" % p], n_x[p])
        send([(xc(p), xc(p), [far_lead], off, sem["xc%d" % p])])
        g.wait_ge(sem["xz%d" % p], n_x[p])
        send([(xz(p), xz(p), [far_lead], off, sem["xz%d" % p])])
        g.wait_ge(sem["xc%d" % rl], n_x[rl])
        send([(xc(rl), xc(rl), [partner], hi, sem["xc%d" % rl])])
        g.wait_ge(sem["xz%d" % rl], n_x[rl])
        send([(xz(rl), xz(rl), [partner], hi, sem["xz%d" % rl])])
        g.wait_ge(sem.cp, len(seq))
        for j in order:
            g.wait_ge(sem["ex%d" % j], n_ex)
        send([(Q[:, 0:16], Q[:, 16:32], [far_lead, far_other], off, sem.st),
              (Q[:, 0:16], Q[:, 0:16], [partner], hi, sem.sl)])
    else:
        send([(xc(r), xc(r), [my_lead], upx, sem["xc%d" % r]), (xc(r), xc(r), [my_helper], uph, sem["xc%d" % r])])
        send([(xz(r), xz(r), [my_lead], upx, sem["xz%d" % r]), (xz(r), xz(r), [my_helper], uph, sem["xz%d" % r])])
        g.wait_ge(sem.qw, 1)
        send([(T.wq[:, 0:NC].bitcast(dt.uint8), T.wq[:, NC:2 * NC].bitcast(dt.uint8), [my_lead], up, sem.wc)])
        send([(T.ws[:, 0:NC], T.ws[:, NC:2 * NC], [my_lead], up, sem.wz)])
    g.wait_ge(sem.ls, sent[0])

    t = g.tensor
    t.wait_ge(sem.qw, 1)
    for j, b in seq:
        if j == r:
            t.wait_ge(sem.qx, 1)
        else:
            t.wait_ge(sem["xc%d" % j], n_x[j])
            t.wait_ge(sem["xz%d" % j], n_x[j])
        if b:
            t.wait_ge(sem.wc, n_w)
            t.wait_ge(sem.wz, n_w)
        t.matmul_mx(bank(j, b), T.xq[:, 128 * j:128 * j + 128], T.xs[:, 128 * j:128 * j + 128],
                    T.wq[:, NC * b:NC * b + NC], T.ws[:, NC * b:NC * b + NC], True, True).then_inc(msem(j, b), 1)

    v = g.vector
    v.memset(T.cv[:, 0:NC - 1], 1.0).then_inc(sem.ms, 1)
    v.memset(T.cv[:, NC - 1:NC], -SCALE).then_inc(sem.ms, 1)
    v.memset(T.R[:, 8:16], 0.0).then_inc(sem.ms, 1)
    v.wait_ge(sem.ldx, 16)
    v.quantize_mx(T.xq[:, 128 * r:128 * r + 128], T.xs[:, 128 * r:128 * r + 128], T.xb[:]).then_inc(sem.qx, 1)
    v.wait_ge(sem.ldw, 16)
    v.quantize_mx(T.wq[:, 0:NC], T.ws[:, 0:NC], T.wb[:]).then_inc(sem.qw, 1)
    v.wait_ge(sem.ms, 3)
    own4 = Q[:, 0:4] if is_lead else T.M4[:]

    def put(k):
        j, b = seq[k]
        v.wait_ge(nsem(j, b), 1)
        dst = Q[:, 4 * b + j:4 * b + j + 1] if is_lead else T.M4[:, j:j + 1]
        v.tensor_copy(dst, shift(k)).then_inc(sem.cp, 1)

    todo = []
    for k, (j, b) in enumerate(seq):
        if k < len(seq) - 1:
            for q in todo:
                put(q)
            todo = []
        v.wait_ge(msem(j, b), 1)
        v.tensor_tensor_scan(T.sc[:, NC * k:NC * k + NC], bank(j, b), T.cv[:], -1.0e29, AluOpType.max, AluOpType.mult
                             ).then_inc(nsem(j, b), 1)
        todo.append(k)
    for q in todo:
        put(q)
    v.wait_ge(sem.cp, len(seq))
    for c in (0, 4, 16, 20):
        v.tensor_copy(T.R[:, c:c + 4], own4).then_inc(sem.rr, 1)
    v.wait_ge(sem.rr, 4)
    for j in order:
        v.wait_ge(sem["ex%d" % j], n_ex)
    if not is_lead:
        v.wait_ge(sem.sl, n_sl)
    v.wait_ge(sem.st, n_st)
    v.tensor_tensor(T.d[:], T.R[:], Q[:, 0:24], AluOpType.subtract).then_inc(sem.v1, 1)
    v.wait_ge(sem.v1, 1)
    v.tensor_scalar(T.D[:], T.d[:], CAP, None, AluOpType.min).then_inc(sem.dd, 1)
    v.wait_ge(sem.ee, 1)
    v.tensor_tensor(T.P[:], T.E[:], Q[:, 8:32], AluOpType.mult).then_inc(sem.p8, 1)
    v.wait_ge(sem.p8, 1)
    v.tensor_tensor(T.U[:], T.P[:, 0:8], T.P[:, 16:24], AluOpType.add).then_inc(sem.u8, 1)
    v.wait_ge(sem.u8, 1)
    v.tensor_tensor(T.S4[:], T.U[:, 0:4], T.U[:, 4:8], AluOpType.add).then_inc(sem.s4, 1)
    v.wait_ge(sem.s4, 1)
    v.reciprocal(T.r4[:], T.S4[:]).then_inc(sem.r4, 1)
    v.wait_ge(sem.r4, 1)
    for j, s in ((0, sem.fin0), (2, sem.fin1)):
        v.tensor_scalar(T.e[:, NC * j:NC * j + NC], T.e[:, NC * j:NC * j + NC], T.r4[:, j:j + 1], None, AluOpType.mult
                        ).then_inc(s, 1)

    a = g.scalar
    for k, (j, b) in enumerate(seq):
        a.wait_ge(nsem(j, b), 1)
        out = (T.junk if b else T.e)[:, NC * j:NC * j + NC]
        if is_lead:
            a.activation(out, bank(j, b), ActivationFunctionType.Exp, bias=shift(k), scale=SCALE,
                         accum_out=Q[:, 8 + 4 * b + j:9 + 4 * b + j]).then_inc(sem["ex%d" % j], 1)
        else:
            a.activation(out, bank(j, b), ActivationFunctionType.Exp, bias=shift(k), scale=SCALE
                         ).then_inc(sem["ex%d" % j], 1)
    a.wait_ge(sem.dd, 1)
    a.activation(T.E[:], T.D[:], ActivationFunctionType.Exp).then_inc(sem.ee, 1)
    a.wait_ge(sem.r4, 1)
    for j, s in ((1, sem.fin0), (3, sem.fin1)):
        a.wait_ge(sem["ex%d" % j], n_ex)
        a.activation(T.e[:, NC * j:NC * j + NC], T.e[:, NC * j:NC * j + NC], ActivationFunctionType.Copy,
                     scale=T.r4[:, j:j + 1]).then_inc(s, 1)

    g.sync.wait_ge(sem.fin0, 2)
    g.sync.dma_start(T.y[:, 0:2 * NC], T.e[:, 0:2 * NC]).then_inc(sem.sto, 16)
    g.sync.wait_ge(sem.fin1, 2)
    g.sync.dma_start(T.y[:, 2 * NC:4 * NC], T.e[:, 2 * NC:4 * NC]).then_inc(sem.sto, 16)
    g.sync.wait_ge(sem.sto, 32)
